import numpy as np
import ml_dtypes

BF16 = ml_dtypes.bfloat16


def bf(x):
    return np.asarray(x, np.float32).astype(BF16)


def f32(x):
    return np.asarray(x, np.float32)


def f64(x):
    return np.asarray(x).astype(np.float64)


def striped(idx):
    return np.tile(idx.reshape(-1, 16).T, (8, 1))


def rows(idx, k):
    return np.tile(idx, (k, 1))


def look(tab, idx):
    return np.take_along_axis(f64(tab), rows(idx, len(tab)), axis=1)


K, S, D, V, N, M = 128, 2048, 2, 512, 1024, 512


def setup_inputs():
    return {"tab": bf(np.random.standard_normal((K, S))), "u": bf(np.random.uniform(0.2, 1.0, (D, K, V))), "w": bf(np.random.standard_normal((K, M)) / np.sqrt(K)), "offs": striped(np.random.permutation(S)[:N])}


def reference(tab, u, w, offs):
    idx = offs[:16].T.reshape(-1)
    x = sum(f64(u[d]) * look(tab, idx[d * V:(d + 1) * V]) for d in range(D))
    y = f64(w).T @ x
    return y

@@ -1,0 +1,51 @@
+import concourse.mybir as mybir
+
+BF16, F32, U16 = mybir.dt.bfloat16, mybir.dt.float32, mybir.dt.uint16
+
+P = 128
+S = 2048
+D = 2
+V = 512
+M = 512
+LIST_COLUMNS = V // 16
+BLOCKS = M // P
+
+FLOPS = 2 * P * M * V + (2 * D - 1) * P * V
+
+
+def tile_lookup_mix_mul_none_kernel(tc, tab, u, w, offs, out):
+    nc = tc.nc
+    mult = mybir.AluOpType.mult
+    with (
+        tc.tile_pool(name="held", bufs=1) as held,
+        tc.psum_pool(name="psum", bufs=1) as psum,
+    ):
+        offsets = held.tile([P, D * LIST_COLUMNS], U16, name="offsets")
+        table = held.tile([P, S], BF16, name="table")
+        weights = held.tile([P, M], BF16, name="weights")
+        factors = [held.tile([P, V], BF16, name=f"factors{d}") for d in range(D)]
+        nc.sync.dma_start(offsets[:], offs)
+        nc.sync.dma_start(table[:], tab)
+        nc.scalar.dma_start(factors[0][:], u[0])
+        nc.scalar.dma_start(weights[:], w)
+        nc.scalar.dma_start(factors[1][:], u[1])
+
+        products = [held.tile([P, V], BF16, name=f"product{d}") for d in range(D)]
+        for d in range(D):
+            picked = table[:].indirect(offsets[:, d * LIST_COLUMNS : (d + 1) * LIST_COLUMNS])
+            nc.vector.tensor_tensor(products[d][:], picked, factors[d][:], mult)
+
+        banks = [psum.tile([P, V], F32, name=f"bank{b}") for b in range(BLOCKS)]
+        for d in range(D):
+            for b in range(BLOCKS):
+                nc.tensor.matmul(
+                    banks[b][:], weights[:, b * P : (b + 1) * P], products[d][:], start=d == 0, stop=d == D - 1
+                )
+
+        for b in range(BLOCKS):
+            staged = held.tile([P, V], F32, name=f"staged{b}")
+            if b % 2 == 0:
+                nc.vector.tensor_copy(staged[:], banks[b][:])
+            else:
+                nc.scalar.copy(staged[:], banks[b][:])
+            nc.sync.dma_start(out[b * P : (b + 1) * P, :], staged[:])

@@ -9,6 +9,7 @@ V = 512
 M = 512
 LIST_COLUMNS = V // 16
 BLOCKS = M // P
+HALF = V // 2
 
 FLOPS = 2 * P * M * V + (2 * D - 1) * P * V
 
@@ -27,25 +28,33 @@ def tile_lookup_mix_mul_none_kernel(tc, tab, u, w, offs, out):
         nc.sync.dma_start(offsets[:], offs)
         nc.sync.dma_start(table[:], tab)
         nc.scalar.dma_start(factors[0][:], u[0])
-        nc.scalar.dma_start(weights[:], w)
-        nc.scalar.dma_start(factors[1][:], u[1])
+        nc.sync.dma_start(factors[1][:], u[1])
+        nc.sync.dma_start(weights[:], w)
+
+        zeros = held.tile([P, HALF], BF16, name="zeros")
+        banks = [[psum.tile([P, HALF], F32, name=f"bank{b}_{h}") for h in range(2)] for b in range(BLOCKS)]
+        nc.vector.memset(zeros[:], 0.0)
+        for n in range(2 * D * BLOCKS):
+            nc.tensor.matmul(banks[-1][-1][:], zeros[:, 0:P], zeros[:], start=True, stop=True)
 
         products = [held.tile([P, V], BF16, name=f"product{d}") for d in range(D)]
         for d in range(D):
             picked = table[:].indirect(offsets[:, d * LIST_COLUMNS : (d + 1) * LIST_COLUMNS])
             nc.vector.tensor_tensor(products[d][:], picked, factors[d][:], mult)
 
-        banks = [psum.tile([P, V], F32, name=f"bank{b}") for b in range(BLOCKS)]
         for d in range(D):
             for b in range(BLOCKS):
-                nc.tensor.matmul(
-                    banks[b][:], weights[:, b * P : (b + 1) * P], products[d][:], start=d == 0, stop=d == D - 1
-                )
+                for h in range(2):
+                    nc.tensor.matmul(
+                        banks[b][h][:],
+                        weights[:, b * P : (b + 1) * P],
+                        products[d][:, h * HALF : (h + 1) * HALF],
+                        start=d == 0,
+                        stop=d == D - 1,
+                    )
 
         for b in range(BLOCKS):
             staged = held.tile([P, V], F32, name=f"staged{b}")
-            if b % 2 == 0:
-                nc.vector.tensor_copy(staged[:], banks[b][:])
-            else:
-                nc.scalar.copy(staged[:], banks[b][:])
+            nc.vector.tensor_copy(staged[:, 0:HALF], banks[b][0][:])
+            nc.scalar.copy(staged[:, HALF:V], banks[b][1][:])
             nc.sync.dma_start(out[b * P : (b + 1) * P, :], staged[:])

@@ -26,7 +26,8 @@ def tile_lookup_mix_mul_none_kernel(tc, tab, u, w, offs, out):
         weights = held.tile([P, M], BF16, name="weights")
         factors = [held.tile([P, V], BF16, name=f"factors{d}") for d in range(D)]
         nc.sync.dma_start(offsets[:], offs)
-        nc.sync.dma_start(table[:], tab)
+        nc.scalar.dma_start(table[:, 0 : S // 2], tab[:, 0 : S // 2])
+        nc.sync.dma_start(table[:, S // 2 : S], tab[:, S // 2 : S])
         nc.scalar.dma_start(factors[0][:], u[0])
         nc.sync.dma_start(factors[1][:], u[1])
         nc.sync.dma_start(weights[:], w)

import concourse.mybir as mybir

BF16, F32, U16 = mybir.dt.bfloat16, mybir.dt.float32, mybir.dt.uint16

P = 128
S = 2048
D = 2
V = 512
M = 512
LIST_COLUMNS = V // 16
BLOCKS = M // P
HALF = V // 2

FLOPS = 2 * P * M * V + (2 * D - 1) * P * V


def tile_lookup_mix_mul_none_kernel(tc, tab, u, w, offs, out):
    nc = tc.nc
    mult = mybir.AluOpType.mult
    with (
        tc.tile_pool(name="held", bufs=1) as held,
        tc.psum_pool(name="psum", bufs=1) as psum,
    ):
        offsets = held.tile([P, D * LIST_COLUMNS], U16, name="offsets")
        table = held.tile([P, S], BF16, name="table")
        weights = held.tile([P, M], BF16, name="weights")
        factors = [held.tile([P, V], BF16, name=f"factors{d}") for d in range(D)]
        nc.sync.dma_start(offsets[:], offs)
        nc.scalar.dma_start(table[:, 0 : S // 2], tab[:, 0 : S // 2])
        nc.sync.dma_start(table[:, S // 2 : S], tab[:, S // 2 : S])
        nc.scalar.dma_start(factors[0][:], u[0])
        nc.sync.dma_start(factors[1][:], u[1])
        nc.sync.dma_start(weights[:], w)

        zeros = held.tile([P, HALF], BF16, name="zeros")
        banks = [[psum.tile([P, HALF], F32, name=f"bank{b}_{h}") for h in range(2)] for b in range(BLOCKS)]
        nc.vector.memset(zeros[:], 0.0)
        for n in range(2 * D * BLOCKS):
            nc.tensor.matmul(banks[-1][-1][:], zeros[:, 0:P], zeros[:], start=True, stop=True)

        products = [held.tile([P, V], BF16, name=f"product{d}") for d in range(D)]
        for d in range(D):
            picked = table[:].indirect(offsets[:, d * LIST_COLUMNS : (d + 1) * LIST_COLUMNS])
            nc.vector.tensor_tensor(products[d][:], picked, factors[d][:], mult)

        for d in range(D):
            for b in range(BLOCKS):
                for h in range(2):
                    nc.tensor.matmul(
                        banks[b][h][:],
                        weights[:, b * P : (b + 1) * P],
                        products[d][:, h * HALF : (h + 1) * HALF],
                        start=d == 0,
                        stop=d == D - 1,
                    )

        for b in range(BLOCKS):
            staged = held.tile([P, V], F32, name=f"staged{b}")
            nc.vector.tensor_copy(staged[:, 0:HALF], banks[b][0][:])
            nc.scalar.copy(staged[:, HALF:V], banks[b][1][:])
            nc.sync.dma_start(out[b * P : (b + 1) * P, :], staged[:])
